import numpy as np
import ml_dtypes


def mxq(x, axis, fmt="e4m3"):
    dtype, down = {"e4m3": (ml_dtypes.float8_e4m3fn, 7), "e5m2": (ml_dtypes.float8_e5m2, 14)}[fmt]
    v = np.moveaxis(np.asarray(x, np.float32).astype(ml_dtypes.bfloat16).astype(np.float64), axis, -1)
    blocks = v.reshape(v.shape[:-1] + (-1, 32))
    amax = np.abs(blocks).max(-1, keepdims=True)
    byte = np.maximum(np.where(amax > 0, np.frexp(amax)[1] - 1 + 127, 0) - down, 1)
    scale = np.exp2(byte - 127.0)
    codes = (blocks / scale).astype(np.float32).astype(dtype).astype(np.float64)
    return np.moveaxis((codes * scale).reshape(v.shape), -1, axis)


WIDE = False


def mx_kscale(k):
    if not WIDE:
        return np.ones(k)
    levels = np.array([10, -10, 5, -5, 0])
    if k % 512:
        return np.exp2(np.random.permutation(np.resize(levels, k // 32))).repeat(32)
    a = np.empty((k // 512, 16))
    for p in range(k // 512):
        a[p, :8] = np.random.permutation(np.resize(levels, 8))
        for g in range(8):
            far = levels[np.abs(levels - a[p, g]) >= 10]
            a[p, g + 8] = far[np.random.randint(len(far))]
    return np.exp2(a.ravel()).repeat(32)


def f64(x):
    return np.asarray(x).astype(np.float64)


def striped8(idx):
    return np.concatenate([v.reshape(-1, 16).T for v in idx]).astype(np.uint16)


def unstriped8(offs):
    return np.stack([offs[16 * g:16 * g + 16].T.reshape(-1) for g in range(8)]).astype(np.int64)


E2M1 = np.array([0.0, 0.5, 1.0, 1.5, 2.0, 3.0, 4.0, 6.0, -0.0, -0.5, -1.0, -1.5, -2.0, -3.0, -4.0, -6.0])


def pack_weight(w, fmt):
    k, n = w.shape
    w = f64(np.asarray(w, np.float32).astype(ml_dtypes.bfloat16)).reshape(k // 32, 32, n)
    amax = np.abs(w).max(1)
    if fmt == "e4m3":
        byte = np.frexp(amax)[1] - 1 + 127 - 7
    else:
        mant, ex = np.frexp(amax / 6.0)
        byte = np.where(mant > 0.5, ex, ex - 1) + 127
    byte = np.clip(np.where(amax > 0, byte, 1), 1, 254)
    scaled = (w * np.exp2(127.0 - byte)[:, None, :]).reshape(k, n).astype(np.float32)
    by_word = np.ascontiguousarray(scaled.reshape(k // 512, 128, 4, n).transpose(0, 1, 3, 2))
    if fmt == "e4m3":
        words = by_word.astype(ml_dtypes.float8_e4m3fn).view(np.uint8)
    else:
        c = by_word.astype(ml_dtypes.float4_e2m1fn).view(np.uint8) & 0xF
        words = (c[..., 0::2] | (c[..., 1::2] << 4)).reshape(k // 512, 128, 2 * n)
    return np.ascontiguousarray(words), np.ascontiguousarray(byte.astype(np.uint8).reshape(k // 512, 16, n))


def unpack_weight(words, scales, fmt):
    g, _, n = scales.shape
    words = np.ascontiguousarray(words).reshape(g, 128, n, -1)
    if fmt == "e4m3":
        vals = words.view(ml_dtypes.float8_e4m3fn).astype(np.float64)
    else:
        nib = np.empty((g, 128, n, 4), np.uint8)
        nib[..., 0::2] = words & 0xF
        nib[..., 1::2] = words >> 4
        vals = E2M1[nib]
    vals = vals * np.repeat(np.exp2(scales.astype(np.float64) - 127.0), 8, axis=1)[..., None]
    return vals.transpose(0, 1, 3, 2).reshape(g * 512, n)


K, M, T, S = 512, 512, 1024, 512


def setup_inputs():
    n = np.random.standard_normal
    s = mx_kscale(K)[:, None]
    p_w = pack_weight(n((K, M)) / np.sqrt(K) / s, "e4m3")
    return {
        "xT": (n((K, T)) * s).astype(np.float32),
        "w_words": p_w[0],
        "w_scales": p_w[1],
        "wgt": np.repeat(np.random.uniform(0.5, 2.0, (8, S)), 16, axis=0).astype(np.float32),
        "offs": striped8(np.stack([np.random.permutation(T)[:S] for _ in range(8)])),
    }


def reference(xT, w_words, w_scales, wgt, offs):
    idx = unstriped8(offs)
    group = np.arange(K) % 512 // 64
    xg = f64(wgt)[np.arange(K) // 4 % 128] * f64(xT)[np.arange(K)[:, None], idx[group]]
    xT_ = mxq(xg, 0, "e4m3")
    w_ = unpack_weight(w_words, w_scales, "e4m3")
    y = xT_.T @ w_
    return y

@@ -1,0 +1,132 @@
+from contextlib import ExitStack
+
+import concourse.mybir as mybir
+
+F32 = mybir.dt.float32
+BF16 = mybir.dt.bfloat16
+I32 = mybir.dt.int32
+U32 = mybir.dt.uint32
+U16 = mybir.dt.uint16
+U8 = mybir.dt.uint8
+FP8X4 = mybir.dt.float8_e4m3fn_x4
+MULT = mybir.AluOpType.mult
+
+P = 128
+PACK = 4
+T = 1024
+S = 512
+N = 512
+TILE = 128
+FLOPS = 2 * 512 * S * N
+
+
+def tile_list_heads_tm_none_kernel(tc, xT, w_words, w_scales, wgt, offs, out):
+    nc = tc.nc
+    planes_hbm = xT.rearrange("(p i) t -> p i t", i=PACK)
+    scales_hbm = w_scales[0].rearrange("(q r) n -> r q n", r=4)
+
+    with ExitStack() as ctx:
+        lists_pool = ctx.enter_context(tc.tile_pool(name="lists_pool", bufs=1))
+        sb = ctx.enter_context(tc.tile_pool(name="sb", bufs=1))
+        ps = ctx.enter_context(tc.psum_pool(name="ps", bufs=1))
+
+        offsets = lists_pool.tile([P, S // 16], U16, name="offsets")
+        nc.sync.dma_start(offsets[:], offs)
+
+        wsc = sb.tile([P, N], U8, name="wsc", align_bytes=64)
+        nc.gpsimd.memset(wsc[:].bitcast(I32), 0)
+
+        weights = sb.tile([P, S], F32, name="weights", align_bytes=64)
+        nc.sync.dma_start(weights[:, 0:TILE], wgt[:, 0:TILE])
+        planes = [sb.tile([P, T], F32, name=f"plane{i}", align_bytes=64) for i in range(PACK)]
+        nc.sync.dma_start(planes[0][:], planes_hbm[:, 0, :])
+        nc.sync.dma_start(weights[:, TILE:S], wgt[:, TILE:S])
+        for i in range(1, PACK):
+            nc.sync.dma_start(planes[i][:], planes_hbm[:, i, :])
+        wcodes = sb.tile([P, N], U32, name="wcodes", align_bytes=64)
+        nc.sync.dma_start(wcodes[:].bitcast(I32), w_words[0].rearrange("p n t -> p (n t)").bitcast(I32))
+        for r in range(4):
+            nc.gpsimd.dma_start(wsc[r:P:32, :].bitcast(I32), scales_hbm[r].bitcast(I32))
+
+        low = sb.tile([P, 2, S], F32, name="low", align_bytes=64)
+        high = [sb.tile([P, 2, TILE], F32, name=f"high{s}", align_bytes=64) for s in range(4)]
+        grouped = [sb.tile([P, TILE, PACK], BF16, name=f"grouped{s}", align_bytes=64) for s in range(4)]
+        codes = [sb.tile([P, TILE], U32, name=f"codes{s}", align_bytes=64) for s in range(4)]
+        scales = [sb.tile([P, TILE], U8, name=f"scales{s}", align_bytes=64) for s in range(4)]
+
+        def gather(dst, i, a, b):
+            nc.vector.tensor_tensor(dst, planes[i][:].indirect(offsets[:, a // 16 : b // 16]), weights[:, a:b], MULT)
+
+        def low_copy(s):
+            nc.scalar.copy(
+                grouped[s][:, :, 0:2],
+                low[:, :, s * TILE : (s + 1) * TILE].rearrange("p i w -> p w i"),
+            )
+
+        def high_copy(copy, s):
+            copy(grouped[s][:, :, 2:4], high[s][:].rearrange("p i w -> p w i"))
+
+        def quantize(s):
+            nc.vector.quantize_mx(
+                out=codes[s][:].bitcast(FP8X4), scales=scales[s][:], in_=grouped[s][:].rearrange("p w i -> p (w i)")
+            )
+
+        def multiply(bank, s, a, b):
+            nc.tensor.matmul_mx(
+                out=bank,
+                lhsT=codes[s][:].bitcast(FP8X4),
+                lhsT_scale=scales[s][:],
+                rhs=wcodes[:, a:b].bitcast(FP8X4),
+                rhs_scale=wsc[:, a:b],
+                start=True,
+                stop=True,
+            )
+
+        def emit(s):
+            bank = ps.tile([P, N], F32, name=f"bank{s}")
+            result = sb.tile([P, N], F32, name=f"result{s}", align_bytes=64)
+            multiply(bank[:], s, 0, N)
+            nc.scalar.copy(result[:], bank[:])
+            nc.sync.dma_start(out[s * TILE : (s + 1) * TILE, :], result[:])
+
+        def emit_last(s):
+            h = N // 2
+            banks = [ps.tile([P, h], F32, name=f"half{b}") for b in range(2)]
+            results = [sb.tile([P, h], F32, name=f"rhalf{b}", align_bytes=64) for b in range(2)]
+            multiply(banks[0][:], s, 0, h)
+            multiply(banks[1][:], s, h, N)
+            nc.vector.tensor_copy(results[0][:], banks[0][:])
+            nc.scalar.copy(results[1][:], banks[1][:])
+            nc.sync.dma_start(out[s * TILE : (s + 1) * TILE, 0:h], results[0][:])
+            nc.scalar.dma_start(out[s * TILE : (s + 1) * TILE, h:N], results[1][:])
+
+        def cols(s):
+            return s * TILE, (s + 1) * TILE
+
+        gather(low[:, 0, 0:TILE], 0, 0, TILE)
+        gather(low[:, 0, TILE:S], 0, TILE, S)
+        gather(low[:, 1, 0 : 2 * TILE], 1, 0, 2 * TILE)
+        low_copy(0)
+        low_copy(1)
+        gather(low[:, 1, 2 * TILE : S], 1, 2 * TILE, S)
+        low_copy(2)
+        low_copy(3)
+        for s in range(3):
+            gather(high[s][:, 0, :], 2, *cols(s))
+        gather(high[0][:, 1, :], 3, *cols(0))
+        high_copy(nc.scalar.copy, 0)
+        gather(high[3][:, 0, :], 2, *cols(3))
+        gather(high[1][:, 1, :], 3, *cols(1))
+        high_copy(nc.scalar.copy, 1)
+        quantize(0)
+        emit(0)
+        gather(high[2][:, 1, :], 3, *cols(2))
+        quantize(1)
+        emit(1)
+        gather(high[3][:, 1, :], 3, *cols(3))
+        high_copy(nc.vector.tensor_copy, 2)
+        high_copy(nc.vector.tensor_copy, 3)
+        quantize(2)
+        emit(2)
+        quantize(3)
+        emit_last(3)

@@ -43,14 +43,15 @@ def tile_list_heads_tm_none_kernel(tc, xT, w_words, w_scales, wgt, offs, out):
         nc.sync.dma_start(weights[:, TILE:S], wgt[:, TILE:S])
         for i in range(1, PACK):
             nc.sync.dma_start(planes[i][:], planes_hbm[:, i, :])
+        for r in range(4):
+            nc.sync.dma_start(wsc[r:P:32, :].bitcast(I32), scales_hbm[r].bitcast(I32))
+
         wcodes = sb.tile([P, N], U32, name="wcodes", align_bytes=64)
         nc.sync.dma_start(wcodes[:].bitcast(I32), w_words[0].rearrange("p n t -> p (n t)").bitcast(I32))
-        for r in range(4):
-            nc.gpsimd.dma_start(wsc[r:P:32, :].bitcast(I32), scales_hbm[r].bitcast(I32))
 
         low = sb.tile([P, 2, S], F32, name="low", align_bytes=64)
-        high = [sb.tile([P, 2, TILE], F32, name=f"high{s}", align_bytes=64) for s in range(4)]
-        grouped = [sb.tile([P, TILE, PACK], BF16, name=f"grouped{s}", align_bytes=64) for s in range(4)]
+        high = sb.tile([P, 2, 3 * TILE], F32, name="high", align_bytes=64)
+        grouped = [sb.tile([P, TILE, PACK], BF16, name=f"grouped{s}", tag=f"work{s}", align_bytes=64) for s in range(4)]
         codes = [sb.tile([P, TILE], U32, name=f"codes{s}", align_bytes=64) for s in range(4)]
         scales = [sb.tile([P, TILE], U8, name=f"scales{s}", align_bytes=64) for s in range(4)]
 
@@ -63,8 +64,8 @@ def tile_list_heads_tm_none_kernel(tc, xT, w_words, w_scales, wgt, offs, out):
                 low[:, :, s * TILE : (s + 1) * TILE].rearrange("p i w -> p w i"),
             )
 
-        def high_copy(copy, s):
-            copy(grouped[s][:, :, 2:4], high[s][:].rearrange("p i w -> p w i"))
+        def high_copy(copy, s, pair):
+            copy(grouped[s][:, :, 2:4], pair.rearrange("p i w -> p w i"))
 
         def quantize(s):
             nc.vector.quantize_mx(
@@ -82,27 +83,20 @@ def tile_list_heads_tm_none_kernel(tc, xT, w_words, w_scales, wgt, offs, out):
                 stop=True,
             )
 
-        def emit(s):
-            bank = ps.tile([P, N], F32, name=f"bank{s}")
-            result = sb.tile([P, N], F32, name=f"result{s}", align_bytes=64)
-            multiply(bank[:], s, 0, N)
-            nc.scalar.copy(result[:], bank[:])
-            nc.sync.dma_start(out[s * TILE : (s + 1) * TILE, :], result[:])
-
-        def emit_last(s):
-            h = N // 2
-            banks = [ps.tile([P, h], F32, name=f"half{b}") for b in range(2)]
-            results = [sb.tile([P, h], F32, name=f"rhalf{b}", align_bytes=64) for b in range(2)]
-            multiply(banks[0][:], s, 0, h)
-            multiply(banks[1][:], s, h, N)
-            nc.vector.tensor_copy(results[0][:], banks[0][:])
-            nc.scalar.copy(results[1][:], banks[1][:])
-            nc.sync.dma_start(out[s * TILE : (s + 1) * TILE, 0:h], results[0][:])
-            nc.scalar.dma_start(out[s * TILE : (s + 1) * TILE, h:N], results[1][:])
+        def emit(s, copies):
+            width = N // len(copies)
+            for c, copy in enumerate(copies):
+                a, b = c * width, (c + 1) * width
+                bank = ps.tile([P, width], F32, name=f"bank{s}_{c}")
+                result = sb.tile([P, width], F32, name=f"result{s}_{c}", align_bytes=64)
+                multiply(bank[:], s, a, b)
+                copy(result[:], bank[:])
+                nc.sync.dma_start(out[s * TILE : (s + 1) * TILE, a:b], result[:])
 
         def cols(s):
             return s * TILE, (s + 1) * TILE
 
+        on_vector, on_scalar = nc.vector.tensor_copy, nc.scalar.copy
         gather(low[:, 0, 0:TILE], 0, 0, TILE)
         gather(low[:, 0, TILE:S], 0, TILE, S)
         gather(low[:, 1, 0 : 2 * TILE], 1, 0, 2 * TILE)
@@ -111,22 +105,19 @@ def tile_list_heads_tm_none_kernel(tc, xT, w_words, w_scales, wgt, offs, out):
         gather(low[:, 1, 2 * TILE : S], 1, 2 * TILE, S)
         low_copy(2)
         low_copy(3)
+        gather(high[:, 0, :], 2, 0, 3 * TILE)
         for s in range(3):
-            gather(high[s][:, 0, :], 2, *cols(s))
-        gather(high[0][:, 1, :], 3, *cols(0))
-        high_copy(nc.scalar.copy, 0)
-        gather(high[3][:, 0, :], 2, *cols(3))
-        gather(high[1][:, 1, :], 3, *cols(1))
-        high_copy(nc.scalar.copy, 1)
+            gather(high[:, 1, s * TILE : (s + 1) * TILE], 3, *cols(s))
+            high_copy(on_scalar, s, high[:, :, s * TILE : (s + 1) * TILE])
         quantize(0)
-        emit(0)
-        gather(high[2][:, 1, :], 3, *cols(2))
+        last = sb.tile([P, 2, TILE], F32, name="last", tag="work0", align_bytes=64)
         quantize(1)
-        emit(1)
-        gather(high[3][:, 1, :], 3, *cols(3))
-        high_copy(nc.vector.tensor_copy, 2)
-        high_copy(nc.vector.tensor_copy, 3)
+        gather(last[:, 0, :], 2, *cols(3))
         quantize(2)
-        emit(2)
+        gather(last[:, 1, :], 3, *cols(3))
+        high_copy(on_vector, 3, last[:])
         quantize(3)
-        emit_last(3)
+        emit(0, [on_scalar])
+        emit(1, [on_scalar])
+        emit(2, [on_vector, on_scalar])
+        emit(3, [on_vector, on_scalar])

@@ -30,6 +30,8 @@ def tile_list_heads_tm_none_kernel(tc, xT, w_words, w_scales, wgt, offs, out):
         sb = ctx.enter_context(tc.tile_pool(name="sb", bufs=1))
         ps = ctx.enter_context(tc.psum_pool(name="ps", bufs=1))
 
+        planes = [sb.tile([P, T], F32, name=f"plane{i}", align_bytes=64) for i in range(PACK)]
+        nc.sync.dma_start(planes[0][:], planes_hbm[:, 0, :])
         offsets = lists_pool.tile([P, S // 16], U16, name="offsets")
         nc.sync.dma_start(offsets[:], offs)
 
@@ -38,8 +40,6 @@ def tile_list_heads_tm_none_kernel(tc, xT, w_words, w_scales, wgt, offs, out):
 
         weights = sb.tile([P, S], F32, name="weights", align_bytes=64)
         nc.sync.dma_start(weights[:, 0:TILE], wgt[:, 0:TILE])
-        planes = [sb.tile([P, T], F32, name=f"plane{i}", align_bytes=64) for i in range(PACK)]
-        nc.sync.dma_start(planes[0][:], planes_hbm[:, 0, :])
         nc.sync.dma_start(weights[:, TILE:S], wgt[:, TILE:S])
         for i in range(1, PACK):
             nc.sync.dma_start(planes[i][:], planes_hbm[:, i, :])
@@ -51,7 +51,10 @@ def tile_list_heads_tm_none_kernel(tc, xT, w_words, w_scales, wgt, offs, out):
 
         low = sb.tile([P, 2, S], F32, name="low", align_bytes=64)
         high = sb.tile([P, 2, 3 * TILE], F32, name="high", align_bytes=64)
-        grouped = [sb.tile([P, TILE, PACK], BF16, name=f"grouped{s}", tag=f"work{s}", align_bytes=64) for s in range(4)]
+        work = sb.tile([P, 2, TILE, PACK], BF16, name="work", align_bytes=64)
+        spare = [sb.tile([P, TILE, PACK], BF16, name=f"spare{s}", align_bytes=64) for s in range(2)]
+        grouped = [work[:, 0], work[:, 1], spare[0][:], spare[1][:]]
+        last = work[:].rearrange("p s w i -> p (s w i)")[:, 2 * TILE : 6 * TILE].bitcast(F32).rearrange("p (i w) -> p i w", i=2)
         codes = [sb.tile([P, TILE], U32, name=f"codes{s}", align_bytes=64) for s in range(4)]
         scales = [sb.tile([P, TILE], U8, name=f"scales{s}", align_bytes=64) for s in range(4)]
 
@@ -69,7 +72,7 @@ def tile_list_heads_tm_none_kernel(tc, xT, w_words, w_scales, wgt, offs, out):
 
         def quantize(s):
             nc.vector.quantize_mx(
-                out=codes[s][:].bitcast(FP8X4), scales=scales[s][:], in_=grouped[s][:].rearrange("p w i -> p (w i)")
+                out=codes[s][:].bitcast(FP8X4), scales=scales[s][:], in_=grouped[s].rearrange("p w i -> p (w i)")
             )
 
         def multiply(bank, s, a, b):
@@ -83,15 +86,16 @@ def tile_list_heads_tm_none_kernel(tc, xT, w_words, w_scales, wgt, offs, out):
                 stop=True,
             )
 
-        def emit(s, copies):
-            width = N // len(copies)
-            for c, copy in enumerate(copies):
-                a, b = c * width, (c + 1) * width
+        def emit(s, parts):
+            a = 0
+            for c, (width, copy) in enumerate(parts):
+                b = a + width
                 bank = ps.tile([P, width], F32, name=f"bank{s}_{c}")
                 result = sb.tile([P, width], F32, name=f"result{s}_{c}", align_bytes=64)
                 multiply(bank[:], s, a, b)
                 copy(result[:], bank[:])
                 nc.sync.dma_start(out[s * TILE : (s + 1) * TILE, a:b], result[:])
+                a = b
 
         def cols(s):
             return s * TILE, (s + 1) * TILE
@@ -106,18 +110,19 @@ def tile_list_heads_tm_none_kernel(tc, xT, w_words, w_scales, wgt, offs, out):
         low_copy(2)
         low_copy(3)
         gather(high[:, 0, :], 2, 0, 3 * TILE)
-        for s in range(3):
-            gather(high[:, 1, s * TILE : (s + 1) * TILE], 3, *cols(s))
-            high_copy(on_scalar, s, high[:, :, s * TILE : (s + 1) * TILE])
+        gather(high[:, 1, 0:TILE], 3, 0, TILE)
+        high_copy(on_scalar, 0, high[:, :, 0:TILE])
+        gather(high[:, 1, TILE : 3 * TILE], 3, TILE, 3 * TILE)
+        high_copy(on_scalar, 1, high[:, :, TILE : 2 * TILE])
+        high_copy(on_scalar, 2, high[:, :, 2 * TILE : 3 * TILE])
         quantize(0)
-        last = sb.tile([P, 2, TILE], F32, name="last", tag="work0", align_bytes=64)
-        quantize(1)
         gather(last[:, 0, :], 2, *cols(3))
-        quantize(2)
+        quantize(1)
         gather(last[:, 1, :], 3, *cols(3))
-        high_copy(on_vector, 3, last[:])
+        quantize(2)
+        high_copy(on_vector, 3, last)
         quantize(3)
-        emit(0, [on_scalar])
-        emit(1, [on_scalar])
-        emit(2, [on_vector, on_scalar])
-        emit(3, [on_vector, on_scalar])
+        emit(0, [(N // 2, on_scalar), (N // 2, on_scalar)])
+        emit(1, [(N, on_scalar)])
+        emit(2, [(N // 2, on_vector), (N // 2, on_scalar)])
+        emit(3, [(N // 2, on_scalar), (N // 4, on_vector), (N // 4, on_vector)])

from contextlib import ExitStack

import concourse.mybir as mybir

F32 = mybir.dt.float32
BF16 = mybir.dt.bfloat16
I32 = mybir.dt.int32
U32 = mybir.dt.uint32
U16 = mybir.dt.uint16
U8 = mybir.dt.uint8
FP8X4 = mybir.dt.float8_e4m3fn_x4
MULT = mybir.AluOpType.mult

P = 128
PACK = 4
T = 1024
S = 512
N = 512
TILE = 128
FLOPS = 2 * 512 * S * N


def tile_list_heads_tm_none_kernel(tc, xT, w_words, w_scales, wgt, offs, out):
    nc = tc.nc
    planes_hbm = xT.rearrange("(p i) t -> p i t", i=PACK)
    scales_hbm = w_scales[0].rearrange("(q r) n -> r q n", r=4)

    with ExitStack() as ctx:
        lists_pool = ctx.enter_context(tc.tile_pool(name="lists_pool", bufs=1))
        sb = ctx.enter_context(tc.tile_pool(name="sb", bufs=1))
        ps = ctx.enter_context(tc.psum_pool(name="ps", bufs=1))

        planes = [sb.tile([P, T], F32, name=f"plane{i}", align_bytes=64) for i in range(PACK)]
        nc.sync.dma_start(planes[0][:], planes_hbm[:, 0, :])
        offsets = lists_pool.tile([P, S // 16], U16, name="offsets")
        nc.sync.dma_start(offsets[:], offs)

        wsc = sb.tile([P, N], U8, name="wsc", align_bytes=64)
        nc.gpsimd.memset(wsc[:].bitcast(I32), 0)

        weights = sb.tile([P, S], F32, name="weights", align_bytes=64)
        nc.sync.dma_start(weights[:, 0:TILE], wgt[:, 0:TILE])
        nc.sync.dma_start(weights[:, TILE:S], wgt[:, TILE:S])
        for i in range(1, PACK):
            nc.sync.dma_start(planes[i][:], planes_hbm[:, i, :])
        for r in range(4):
            nc.sync.dma_start(wsc[r:P:32, :].bitcast(I32), scales_hbm[r].bitcast(I32))

        wcodes = sb.tile([P, N], U32, name="wcodes", align_bytes=64)
        nc.sync.dma_start(wcodes[:].bitcast(I32), w_words[0].rearrange("p n t -> p (n t)").bitcast(I32))

        low = sb.tile([P, 2, S], F32, name="low", align_bytes=64)
        high = sb.tile([P, 2, 3 * TILE], F32, name="high", align_bytes=64)
        work = sb.tile([P, 2, TILE, PACK], BF16, name="work", align_bytes=64)
        spare = [sb.tile([P, TILE, PACK], BF16, name=f"spare{s}", align_bytes=64) for s in range(2)]
        grouped = [work[:, 0], work[:, 1], spare[0][:], spare[1][:]]
        last = work[:].rearrange("p s w i -> p (s w i)")[:, 2 * TILE : 6 * TILE].bitcast(F32).rearrange("p (i w) -> p i w", i=2)
        codes = [sb.tile([P, TILE], U32, name=f"codes{s}", align_bytes=64) for s in range(4)]
        scales = [sb.tile([P, TILE], U8, name=f"scales{s}", align_bytes=64) for s in range(4)]

        def gather(dst, i, a, b):
            nc.vector.tensor_tensor(dst, planes[i][:].indirect(offsets[:, a // 16 : b // 16]), weights[:, a:b], MULT)

        def low_copy(s):
            nc.scalar.copy(
                grouped[s][:, :, 0:2],
                low[:, :, s * TILE : (s + 1) * TILE].rearrange("p i w -> p w i"),
            )

        def high_copy(copy, s, pair):
            copy(grouped[s][:, :, 2:4], pair.rearrange("p i w -> p w i"))

        def quantize(s):
            nc.vector.quantize_mx(
                out=codes[s][:].bitcast(FP8X4), scales=scales[s][:], in_=grouped[s].rearrange("p w i -> p (w i)")
            )

        def multiply(bank, s, a, b):
            nc.tensor.matmul_mx(
                out=bank,
                lhsT=codes[s][:].bitcast(FP8X4),
                lhsT_scale=scales[s][:],
                rhs=wcodes[:, a:b].bitcast(FP8X4),
                rhs_scale=wsc[:, a:b],
                start=True,
                stop=True,
            )

        def emit(s, parts):
            a = 0
            for c, (width, copy) in enumerate(parts):
                b = a + width
                bank = ps.tile([P, width], F32, name=f"bank{s}_{c}")
                result = sb.tile([P, width], F32, name=f"result{s}_{c}", align_bytes=64)
                multiply(bank[:], s, a, b)
                copy(result[:], bank[:])
                nc.sync.dma_start(out[s * TILE : (s + 1) * TILE, a:b], result[:])
                a = b

        def cols(s):
            return s * TILE, (s + 1) * TILE

        on_vector, on_scalar = nc.vector.tensor_copy, nc.scalar.copy
        gather(low[:, 0, 0:TILE], 0, 0, TILE)
        gather(low[:, 0, TILE:S], 0, TILE, S)
        gather(low[:, 1, 0 : 2 * TILE], 1, 0, 2 * TILE)
        low_copy(0)
        low_copy(1)
        gather(low[:, 1, 2 * TILE : S], 1, 2 * TILE, S)
        low_copy(2)
        low_copy(3)
        gather(high[:, 0, :], 2, 0, 3 * TILE)
        gather(high[:, 1, 0:TILE], 3, 0, TILE)
        high_copy(on_scalar, 0, high[:, :, 0:TILE])
        gather(high[:, 1, TILE : 3 * TILE], 3, TILE, 3 * TILE)
        high_copy(on_scalar, 1, high[:, :, TILE : 2 * TILE])
        high_copy(on_scalar, 2, high[:, :, 2 * TILE : 3 * TILE])
        quantize(0)
        gather(last[:, 0, :], 2, *cols(3))
        quantize(1)
        gather(last[:, 1, :], 3, *cols(3))
        quantize(2)
        high_copy(on_vector, 3, last)
        quantize(3)
        emit(0, [(N // 2, on_scalar), (N // 2, on_scalar)])
        emit(1, [(N, on_scalar)])
        emit(2, [(N // 2, on_vector), (N // 2, on_scalar)])
        emit(3, [(N // 2, on_scalar), (N // 4, on_vector), (N // 4, on_vector)])
